import numpy as np
import ml_dtypes


def mxq(x, axis, fmt="e4m3"):
    dtype, down = {"e4m3": (ml_dtypes.float8_e4m3fn, 7), "e5m2": (ml_dtypes.float8_e5m2, 14)}[fmt]
    v = np.moveaxis(np.asarray(x, np.float32).astype(ml_dtypes.bfloat16).astype(np.float64), axis, -1)
    blocks = v.reshape(v.shape[:-1] + (-1, 32))
    amax = np.abs(blocks).max(-1, keepdims=True)
    byte = np.maximum(np.where(amax > 0, np.frexp(amax)[1] - 1 + 127, 0) - down, 1)
    scale = np.exp2(byte - 127.0)
    codes = (blocks / scale).astype(np.float32).astype(dtype).astype(np.float64)
    return np.moveaxis((codes * scale).reshape(v.shape), -1, axis)


WIDE = False


def mx_kscale(k):
    if not WIDE:
        return np.ones(k)
    levels = np.array([10, -10, 5, -5, 0])
    if k % 512:
        return np.exp2(np.random.permutation(np.resize(levels, k // 32))).repeat(32)
    a = np.empty((k // 512, 16))
    for p in range(k // 512):
        a[p, :8] = np.random.permutation(np.resize(levels, 8))
        for g in range(8):
            far = levels[np.abs(levels - a[p, g]) >= 10]
            a[p, g + 8] = far[np.random.randint(len(far))]
    return np.exp2(a.ravel()).repeat(32)


def f64(x):
    return np.asarray(x).astype(np.float64)


def striped(idx):
    return np.tile(idx.reshape(-1, 16).T, (8, 1)).astype(np.uint16)


def unstriped(offs):
    return offs[:16].T.reshape(-1).astype(np.int64)


E2M1 = np.array([0.0, 0.5, 1.0, 1.5, 2.0, 3.0, 4.0, 6.0, -0.0, -0.5, -1.0, -1.5, -2.0, -3.0, -4.0, -6.0])


def pack_weight(w, fmt):
    k, n = w.shape
    w = f64(np.asarray(w, np.float32).astype(ml_dtypes.bfloat16)).reshape(k // 32, 32, n)
    amax = np.abs(w).max(1)
    if fmt == "e4m3":
        byte = np.frexp(amax)[1] - 1 + 127 - 7
    else:
        mant, ex = np.frexp(amax / 6.0)
        byte = np.where(mant > 0.5, ex, ex - 1) + 127
    byte = np.clip(np.where(amax > 0, byte, 1), 1, 254)
    scaled = (w * np.exp2(127.0 - byte)[:, None, :]).reshape(k, n).astype(np.float32)
    by_word = np.ascontiguousarray(scaled.reshape(k // 512, 128, 4, n).transpose(0, 1, 3, 2))
    if fmt == "e4m3":
        words = by_word.astype(ml_dtypes.float8_e4m3fn).view(np.uint8)
    else:
        c = by_word.astype(ml_dtypes.float4_e2m1fn).view(np.uint8) & 0xF
        words = (c[..., 0::2] | (c[..., 1::2] << 4)).reshape(k // 512, 128, 2 * n)
    return np.ascontiguousarray(words), np.ascontiguousarray(byte.astype(np.uint8).reshape(k // 512, 16, n))


def unpack_weight(words, scales, fmt):
    g, _, n = scales.shape
    words = np.ascontiguousarray(words).reshape(g, 128, n, -1)
    if fmt == "e4m3":
        vals = words.view(ml_dtypes.float8_e4m3fn).astype(np.float64)
    else:
        nib = np.empty((g, 128, n, 4), np.uint8)
        nib[..., 0::2] = words & 0xF
        nib[..., 1::2] = words >> 4
        vals = E2M1[nib]
    vals = vals * np.repeat(np.exp2(scales.astype(np.float64) - 127.0), 8, axis=1)[..., None]
    return vals.transpose(0, 1, 3, 2).reshape(g * 512, n)


def pack_table4(v):
    words, scales = pack_weight(v, "e2m1")
    g, t = words.shape[0] // 2, v.shape[1]
    words = words.reshape(g, 2, 128, t, 2).transpose(0, 2, 3, 1, 4)
    return np.concatenate([words.reshape(g, -1), scales.reshape(g, -1)], axis=1)


def unpack_table4(tab):
    g, t = tab.shape[0], tab.shape[1] // 544
    words = tab[:, :512 * t].reshape(g, 128, t, 2, 2).transpose(0, 3, 1, 2, 4).reshape(2 * g, 128, 2 * t)
    return unpack_weight(words, tab[:, 512 * t:].reshape(2 * g, 16, t), "e2m1")


def pack_table(v):
    words, scales = pack_weight(v, "e4m3")
    return np.concatenate([words.reshape(words.shape[0], -1), scales.reshape(scales.shape[0], -1)], axis=1)


def unpack_table(tab):
    g, t = tab.shape[0], tab.shape[1] // 528
    return unpack_weight(tab[:, :512 * t].reshape(g, 128, t, 4), tab[:, 512 * t:].reshape(g, 16, t), "e4m3")


def silu(v):
    return v / (1.0 + np.exp(-np.maximum(v, -700.0)))


K, L, M, T, S = 512, 2048, 128, 4096, 1536


def setup_inputs():
    n = np.random.standard_normal
    s1 = mx_kscale(K)[:, None]
    s2 = mx_kscale(L)[:, None]
    p_w4 = pack_weight(n((K, M)) / np.sqrt(K) / s1, "e2m1")
    return {
        "tab": pack_table(n((K, T)) * s1),
        "w4_words": p_w4[0],
        "w4_scales": p_w4[1],
        "tab2": pack_table4(n((L, T)) * s2),
        "u": (n((L, M)) / np.sqrt(L) / s2).astype(np.float32),
        "b": (0.3 * n(128)).astype(np.float32),
        "offs": striped(np.random.permutation(T)[:S]),
        "offs2": striped(np.random.permutation(T)[:S]),
    }


def reference(tab, w4_words, w4_scales, tab2, u, b, offs, offs2):
    tab_ = unpack_table(tab)[:, unstriped(offs)]
    w4_ = unpack_weight(w4_words, w4_scales, "e2m1")
    tab2_ = unpack_table4(tab2)[:, unstriped(offs2)]
    u_ = mxq(f64(u), 0, "e4m3")
    y = tab_.T @ w4_ + tab2_.T @ u_
    return silu(y + f64(b)[None, :])

@@ -1,0 +1,162 @@
+from contextlib import ExitStack
+
+import concourse.mybir as mybir
+from concourse.masks import make_identity
+
+K, L, N, T, S = 512, 2048, 128, 4096, 1536
+FLOPS = 2 * S * N * (K + L)
+
+F32 = mybir.dt.float32
+BF16 = mybir.dt.bfloat16
+I32 = mybir.dt.int32
+U32 = mybir.dt.uint32
+U16 = mybir.dt.uint16
+U8 = mybir.dt.uint8
+FP8X4 = mybir.dt.float8_e4m3fn_x4
+FP4X4 = mybir.dt.float4_e2m1fn_x4
+SILU = mybir.ActivationFunctionType.Silu
+
+P = 128
+WORDS = 512 * T
+SLICE = 512
+COLS = S // 16
+
+
+def tile_list_tab48_tm_silu_kernel(tc, tab, w4_words, w4_scales, tab2, u, b, offs, offs2, out):
+    nc = tc.nc
+    with ExitStack() as ctx:
+        lists = ctx.enter_context(tc.tile_pool(name="lists", bufs=1))
+        keep = ctx.enter_context(tc.tile_pool(name="keep", bufs=1))
+        psum = ctx.enter_context(tc.psum_pool(name="psum", bufs=1))
+
+        list2 = lists.tile([P, COLS], U16, name="list2")
+        list1 = lists.tile([P, COLS], U16, name="list1")
+        win2 = keep.tile([P, T // 4], I32, name="win2")
+        win1 = keep.tile([P, T // 4], I32, name="win1")
+
+        nc.sync.dma_start(list2[:], offs2)
+        for m in range(2):
+            nc.sync.dma_start(
+                out=win2[64 * m : 64 * m + 32, :],
+                in_=tab2[m : m + 1, WORDS:].bitcast(I32).rearrange("o (q c) -> (o q) c", c=T // 4),
+            )
+        nc.gpsimd.memset(win2[32:64, :], 0)
+        nc.gpsimd.memset(win2[96:128, :], 0)
+        nc.vector.memset(win1[:], 0)
+        nc.sync.dma_start(list1[:], offs)
+        scales1 = tab[0:1, WORDS:].bitcast(I32).rearrange("o (q c) -> (o q) c", c=T // 4)
+        for q in range(4):
+            nc.scalar.dma_start(out=win1[32 * q : 32 * q + 4, :], in_=scales1[4 * q : 4 * q + 4, :])
+
+        words = [keep.tile([P, T], I32, name=f"words{m}") for m in range(2)]
+        words1 = keep.tile([P, T], I32, name="words_tab")
+        raw = keep.tile([P, 4, 4, N], F32, name="raw")
+        nc.sync.dma_start(out=words[0][:], in_=tab2[0:1, :WORDS].bitcast(I32).rearrange("o (p t) -> (o p) t", p=P))
+        nc.sync.dma_start(out=raw[:].rearrange("p a i n -> p a (i n)"), in_=u.rearrange("(a p i) n -> p a (i n)", a=4, i=4))
+        nc.sync.dma_start(out=words[1][:], in_=tab2[1:2, :WORDS].bitcast(I32).rearrange("o (p t) -> (o p) t", p=P))
+        nc.sync.dma_start(out=words1[:], in_=tab[0:1, :WORDS].bitcast(I32).rearrange("o (p t) -> (o p) t", p=P))
+
+        planes = [keep.tile([P, S], U8, name=f"plane2_{a}", align_bytes=64) for a in range(4)]
+        for a in range(4):
+            nc.gpsimd.memset(planes[a][:].bitcast(I32), 0)
+        w_codes = keep.tile([P, 2 * N], U8, name="w_codes", align_bytes=64)
+        w_scales = keep.tile([P, N], U8, name="w_scales", align_bytes=64)
+        b_col = keep.tile([P, 1], F32, name="b_col")
+        nc.gpsimd.memset(w_scales[:].bitcast(I32), 0)
+        ident = keep.tile([P, P], F32, name="ident")
+        make_identity(nc, ident[:])
+        warm = keep.tile([P, 1], F32, name="warm")
+        nc.scalar.activation(warm[:], ident[:, 0:1], SILU)
+
+        got2 = keep.tile([P, S], U8, name="got2", align_bytes=64)
+        nc.vector.tensor_copy(got2[:], win2[:].bitcast(U8).indirect(list2[:]))
+        for a in range(4):
+            queue = nc.sync if a < 2 else nc.gpsimd
+            for q in range(4):
+                row = 64 * (a // 2) + 16 * (a % 2) + 4 * q
+                queue.dma_start(
+                    out=planes[a][32 * q : 32 * q + 4, :].bitcast(I32), in_=got2[row : row + 4, :].bitcast(I32)
+                )
+        plane1 = keep.tile([P, S], U8, name="plane1", align_bytes=64)
+        nc.vector.tensor_copy(plane1[:], win1[:].bitcast(U8).indirect(list1[:]))
+
+        nc.gpsimd.dma_start(out=w_codes[:].bitcast(I32), in_=w4_words[0].bitcast(I32))
+        for q in range(4):
+            nc.gpsimd.dma_start(
+                out=w_scales[32 * q : 32 * q + 4, :].bitcast(I32), in_=w4_scales[0, 4 * q : 4 * q + 4, :].bitcast(I32)
+            )
+        nc.gpsimd.dma_start(out=b_col[:], in_=b.rearrange("(p o) -> p o", o=1))
+
+        grouped = keep.tile([P, 4, N, 4], BF16, name="grouped", align_bytes=64)
+        nc.scalar.copy(out=grouped[:], in_=raw[:].rearrange("p a i n -> p a n i"))
+        u_codes = keep.tile([P, 4 * N], U32, name="u_codes", align_bytes=64)
+        u_scales = keep.tile([P, 4 * N], U8, name="u_scales", align_bytes=64)
+
+        parted = [keep.tile([P, 4 * S], U8, name=f"parted{m}", align_bytes=64) for m in range(2)]
+        got = [keep.tile([P, S], U32, name=f"got_{m}", align_bytes=64) for m in range(2)]
+        codes1 = keep.tile([P, S], U32, name="codes1", align_bytes=64)
+
+        def part(m):
+            nc.vector.tensor_copy(
+                parted[m][:].bitcast(U16).rearrange("p (h j) -> p h j", h=2),
+                got[m][:].bitcast(U16).rearrange("p (j h) -> p h j", h=2),
+            )
+
+        acc = [psum.tile([P, SLICE], F32, name=f"acc{s}") for s in range(3)]
+
+        def pass2(a):
+            for s in range(3):
+                first = (a % 2) * 2 * S + 2 * SLICE * s
+                nc.tensor.matmul_mx(
+                    out=acc[s][:],
+                    lhsT=u_codes[:, N * a : N * (a + 1)].bitcast(FP8X4),
+                    lhsT_scale=u_scales[:, N * a : N * (a + 1)],
+                    rhs=parted[a // 2][:, first : first + 2 * SLICE].bitcast(FP4X4),
+                    rhs_scale=planes[a][:, SLICE * s : SLICE * (s + 1)],
+                    start=(a == 0),
+                    stop=False,
+                )
+
+        def pass1(s):
+            nc.tensor.matmul_mx(
+                out=acc[s][:],
+                lhsT=w_codes[:].bitcast(FP4X4),
+                lhsT_scale=w_scales[:],
+                rhs=codes1[:, SLICE * s : SLICE * (s + 1)].bitcast(FP8X4),
+                rhs_scale=plane1[:, SLICE * s : SLICE * (s + 1)],
+                start=False,
+                stop=True,
+            )
+
+        nc.vector.tensor_copy(got[0][:], words[0][:].bitcast(U32).indirect(list2[:]))
+        nc.vector.quantize_mx(
+            out=u_codes[:].bitcast(FP8X4), scales=u_scales[:], in_=grouped[:].rearrange("p a n i -> p (a n i)")
+        )
+        part(0)
+        nc.vector.tensor_copy(got[1][:], words[1][:].bitcast(U32).indirect(list2[:]))
+        pass2(0)
+        pass2(1)
+        part(1)
+        pass2(2)
+        pass2(3)
+
+        def finish(s, copy_out):
+            for h in range(2):
+                cols = slice(256 * h, 256 * (h + 1))
+                act = keep.tile([P, 256], F32, name=f"act{s}_{h}")
+                nc.scalar.activation(act[:], acc[s][:, cols], SILU, bias=b_col[:])
+                turned = psum.tile([P, 2, N], F32, name=f"turned{(s % 2)}_{h}")
+                for t in range(2):
+                    nc.tensor.transpose(turned[:, t, :], act[:, 128 * t : 128 * (t + 1)], ident[:])
+                res = keep.tile([P, 2, N], F32, name=f"res{s}_{h}")
+                copy_out(res[:], turned[:])
+                rows = out[SLICE * s + 256 * h : SLICE * s + 256 * (h + 1), :]
+                nc.sync.dma_start(out=rows.rearrange("(t p) n -> p t n", p=P), in_=res[:])
+
+        for s in range(3):
+            nc.vector.tensor_copy(
+                codes1[:, SLICE * s : SLICE * (s + 1)],
+                words1[:].bitcast(U32).indirect(list1[:, SLICE // 16 * s : SLICE // 16 * (s + 1)]),
+            )
+            pass1(s)
+            finish(s, nc.vector.tensor_copy if s == 2 else nc.scalar.copy)

@@ -40,21 +40,19 @@ def tile_list_tab48_tm_silu_kernel(tc, tab, w4_words, w4_scales, tab2, u, b, off
                 out=win2[64 * m : 64 * m + 32, :],
                 in_=tab2[m : m + 1, WORDS:].bitcast(I32).rearrange("o (q c) -> (o q) c", c=T // 4),
             )
-        nc.gpsimd.memset(win2[32:64, :], 0)
-        nc.gpsimd.memset(win2[96:128, :], 0)
         nc.vector.memset(win1[:], 0)
+        nc.vector.memset(win2[32:64, :], 0)
+        nc.vector.memset(win2[96:128, :], 0)
         nc.sync.dma_start(list1[:], offs)
         scales1 = tab[0:1, WORDS:].bitcast(I32).rearrange("o (q c) -> (o q) c", c=T // 4)
         for q in range(4):
             nc.scalar.dma_start(out=win1[32 * q : 32 * q + 4, :], in_=scales1[4 * q : 4 * q + 4, :])
 
-        words = [keep.tile([P, T], I32, name=f"words{m}") for m in range(2)]
-        words1 = keep.tile([P, T], I32, name="words_tab")
+        words = [keep.tile([P, T], I32, name=f"words{m}", tag=f"words{m}") for m in range(2)]
         raw = keep.tile([P, 4, 4, N], F32, name="raw")
         nc.sync.dma_start(out=words[0][:], in_=tab2[0:1, :WORDS].bitcast(I32).rearrange("o (p t) -> (o p) t", p=P))
         nc.sync.dma_start(out=raw[:].rearrange("p a i n -> p a (i n)"), in_=u.rearrange("(a p i) n -> p a (i n)", a=4, i=4))
         nc.sync.dma_start(out=words[1][:], in_=tab2[1:2, :WORDS].bitcast(I32).rearrange("o (p t) -> (o p) t", p=P))
-        nc.sync.dma_start(out=words1[:], in_=tab[0:1, :WORDS].bitcast(I32).rearrange("o (p t) -> (o p) t", p=P))
 
         planes = [keep.tile([P, S], U8, name=f"plane2_{a}", align_bytes=64) for a in range(4)]
         for a in range(4):
@@ -68,24 +66,23 @@ def tile_list_tab48_tm_silu_kernel(tc, tab, w4_words, w4_scales, tab2, u, b, off
         warm = keep.tile([P, 1], F32, name="warm")
         nc.scalar.activation(warm[:], ident[:, 0:1], SILU)
 
+        nc.scalar.dma_start(out=w_codes[:].bitcast(I32), in_=w4_words[0].bitcast(I32))
+        for q in range(4):
+            nc.scalar.dma_start(
+                out=w_scales[32 * q : 32 * q + 4, :].bitcast(I32), in_=w4_scales[0, 4 * q : 4 * q + 4, :].bitcast(I32)
+            )
+        nc.scalar.dma_start(out=b_col[:], in_=b.rearrange("(p o) -> p o", o=1))
+
         got2 = keep.tile([P, S], U8, name="got2", align_bytes=64)
         nc.vector.tensor_copy(got2[:], win2[:].bitcast(U8).indirect(list2[:]))
         for a in range(4):
-            queue = nc.sync if a < 2 else nc.gpsimd
             for q in range(4):
                 row = 64 * (a // 2) + 16 * (a % 2) + 4 * q
-                queue.dma_start(
+                nc.sync.dma_start(
                     out=planes[a][32 * q : 32 * q + 4, :].bitcast(I32), in_=got2[row : row + 4, :].bitcast(I32)
                 )
         plane1 = keep.tile([P, S], U8, name="plane1", align_bytes=64)
         nc.vector.tensor_copy(plane1[:], win1[:].bitcast(U8).indirect(list1[:]))
-
-        nc.gpsimd.dma_start(out=w_codes[:].bitcast(I32), in_=w4_words[0].bitcast(I32))
-        for q in range(4):
-            nc.gpsimd.dma_start(
-                out=w_scales[32 * q : 32 * q + 4, :].bitcast(I32), in_=w4_scales[0, 4 * q : 4 * q + 4, :].bitcast(I32)
-            )
-        nc.gpsimd.dma_start(out=b_col[:], in_=b.rearrange("(p o) -> p o", o=1))
 
         grouped = keep.tile([P, 4, N, 4], BF16, name="grouped", align_bytes=64)
         nc.scalar.copy(out=grouped[:], in_=raw[:].rearrange("p a i n -> p a n i"))
@@ -134,6 +131,8 @@ def tile_list_tab48_tm_silu_kernel(tc, tab, w4_words, w4_scales, tab2, u, b, off
         )
         part(0)
         nc.vector.tensor_copy(got[1][:], words[1][:].bitcast(U32).indirect(list2[:]))
+        words1 = keep.tile([P, T], I32, name="words_tab", tag="words0")
+        nc.sync.dma_start(out=words1[:], in_=tab[0:1, :WORDS].bitcast(I32).rearrange("o (p t) -> (o p) t", p=P))
         pass2(0)
         pass2(1)
         part(1)

from contextlib import ExitStack

import concourse.mybir as mybir
from concourse.masks import make_identity

K, L, N, T, S = 512, 2048, 128, 4096, 1536
FLOPS = 2 * S * N * (K + L)

F32 = mybir.dt.float32
BF16 = mybir.dt.bfloat16
I32 = mybir.dt.int32
U32 = mybir.dt.uint32
U16 = mybir.dt.uint16
U8 = mybir.dt.uint8
FP8X4 = mybir.dt.float8_e4m3fn_x4
FP4X4 = mybir.dt.float4_e2m1fn_x4
SILU = mybir.ActivationFunctionType.Silu

P = 128
WORDS = 512 * T
SLICE = 512
COLS = S // 16


def tile_list_tab48_tm_silu_kernel(tc, tab, w4_words, w4_scales, tab2, u, b, offs, offs2, out):
    nc = tc.nc
    with ExitStack() as ctx:
        lists = ctx.enter_context(tc.tile_pool(name="lists", bufs=1))
        keep = ctx.enter_context(tc.tile_pool(name="keep", bufs=1))
        psum = ctx.enter_context(tc.psum_pool(name="psum", bufs=1))

        list2 = lists.tile([P, COLS], U16, name="list2")
        list1 = lists.tile([P, COLS], U16, name="list1")
        win2 = keep.tile([P, T // 4], I32, name="win2")
        win1 = keep.tile([P, T // 4], I32, name="win1")

        nc.sync.dma_start(list2[:], offs2)
        for m in range(2):
            nc.sync.dma_start(
                out=win2[64 * m : 64 * m + 32, :],
                in_=tab2[m : m + 1, WORDS:].bitcast(I32).rearrange("o (q c) -> (o q) c", c=T // 4),
            )
        nc.vector.memset(win1[:], 0)
        nc.vector.memset(win2[32:64, :], 0)
        nc.vector.memset(win2[96:128, :], 0)
        nc.sync.dma_start(list1[:], offs)
        scales1 = tab[0:1, WORDS:].bitcast(I32).rearrange("o (q c) -> (o q) c", c=T // 4)
        for q in range(4):
            nc.scalar.dma_start(out=win1[32 * q : 32 * q + 4, :], in_=scales1[4 * q : 4 * q + 4, :])

        words = [keep.tile([P, T], I32, name=f"words{m}", tag=f"words{m}") for m in range(2)]
        raw = keep.tile([P, 4, 4, N], F32, name="raw")
        nc.sync.dma_start(out=words[0][:], in_=tab2[0:1, :WORDS].bitcast(I32).rearrange("o (p t) -> (o p) t", p=P))
        nc.sync.dma_start(out=raw[:].rearrange("p a i n -> p a (i n)"), in_=u.rearrange("(a p i) n -> p a (i n)", a=4, i=4))
        nc.sync.dma_start(out=words[1][:], in_=tab2[1:2, :WORDS].bitcast(I32).rearrange("o (p t) -> (o p) t", p=P))

        planes = [keep.tile([P, S], U8, name=f"plane2_{a}", align_bytes=64) for a in range(4)]
        for a in range(4):
            nc.gpsimd.memset(planes[a][:].bitcast(I32), 0)
        w_codes = keep.tile([P, 2 * N], U8, name="w_codes", align_bytes=64)
        w_scales = keep.tile([P, N], U8, name="w_scales", align_bytes=64)
        b_col = keep.tile([P, 1], F32, name="b_col")
        nc.gpsimd.memset(w_scales[:].bitcast(I32), 0)
        ident = keep.tile([P, P], F32, name="ident")
        make_identity(nc, ident[:])
        warm = keep.tile([P, 1], F32, name="warm")
        nc.scalar.activation(warm[:], ident[:, 0:1], SILU)

        nc.scalar.dma_start(out=w_codes[:].bitcast(I32), in_=w4_words[0].bitcast(I32))
        for q in range(4):
            nc.scalar.dma_start(
                out=w_scales[32 * q : 32 * q + 4, :].bitcast(I32), in_=w4_scales[0, 4 * q : 4 * q + 4, :].bitcast(I32)
            )
        nc.scalar.dma_start(out=b_col[:], in_=b.rearrange("(p o) -> p o", o=1))

        got2 = keep.tile([P, S], U8, name="got2", align_bytes=64)
        nc.vector.tensor_copy(got2[:], win2[:].bitcast(U8).indirect(list2[:]))
        for a in range(4):
            for q in range(4):
                row = 64 * (a // 2) + 16 * (a % 2) + 4 * q
                nc.sync.dma_start(
                    out=planes[a][32 * q : 32 * q + 4, :].bitcast(I32), in_=got2[row : row + 4, :].bitcast(I32)
                )
        plane1 = keep.tile([P, S], U8, name="plane1", align_bytes=64)
        nc.vector.tensor_copy(plane1[:], win1[:].bitcast(U8).indirect(list1[:]))

        grouped = keep.tile([P, 4, N, 4], BF16, name="grouped", align_bytes=64)
        nc.scalar.copy(out=grouped[:], in_=raw[:].rearrange("p a i n -> p a n i"))
        u_codes = keep.tile([P, 4 * N], U32, name="u_codes", align_bytes=64)
        u_scales = keep.tile([P, 4 * N], U8, name="u_scales", align_bytes=64)

        parted = [keep.tile([P, 4 * S], U8, name=f"parted{m}", align_bytes=64) for m in range(2)]
        got = [keep.tile([P, S], U32, name=f"got_{m}", align_bytes=64) for m in range(2)]
        codes1 = keep.tile([P, S], U32, name="codes1", align_bytes=64)

        def part(m):
            nc.vector.tensor_copy(
                parted[m][:].bitcast(U16).rearrange("p (h j) -> p h j", h=2),
                got[m][:].bitcast(U16).rearrange("p (j h) -> p h j", h=2),
            )

        acc = [psum.tile([P, SLICE], F32, name=f"acc{s}") for s in range(3)]

        def pass2(a):
            for s in range(3):
                first = (a % 2) * 2 * S + 2 * SLICE * s
                nc.tensor.matmul_mx(
                    out=acc[s][:],
                    lhsT=u_codes[:, N * a : N * (a + 1)].bitcast(FP8X4),
                    lhsT_scale=u_scales[:, N * a : N * (a + 1)],
                    rhs=parted[a // 2][:, first : first + 2 * SLICE].bitcast(FP4X4),
                    rhs_scale=planes[a][:, SLICE * s : SLICE * (s + 1)],
                    start=(a == 0),
                    stop=False,
                )

        def pass1(s):
            nc.tensor.matmul_mx(
                out=acc[s][:],
                lhsT=w_codes[:].bitcast(FP4X4),
                lhsT_scale=w_scales[:],
                rhs=codes1[:, SLICE * s : SLICE * (s + 1)].bitcast(FP8X4),
                rhs_scale=plane1[:, SLICE * s : SLICE * (s + 1)],
                start=False,
                stop=True,
            )

        nc.vector.tensor_copy(got[0][:], words[0][:].bitcast(U32).indirect(list2[:]))
        nc.vector.quantize_mx(
            out=u_codes[:].bitcast(FP8X4), scales=u_scales[:], in_=grouped[:].rearrange("p a n i -> p (a n i)")
        )
        part(0)
        nc.vector.tensor_copy(got[1][:], words[1][:].bitcast(U32).indirect(list2[:]))
        words1 = keep.tile([P, T], I32, name="words_tab", tag="words0")
        nc.sync.dma_start(out=words1[:], in_=tab[0:1, :WORDS].bitcast(I32).rearrange("o (p t) -> (o p) t", p=P))
        pass2(0)
        pass2(1)
        part(1)
        pass2(2)
        pass2(3)

        def finish(s, copy_out):
            for h in range(2):
                cols = slice(256 * h, 256 * (h + 1))
                act = keep.tile([P, 256], F32, name=f"act{s}_{h}")
                nc.scalar.activation(act[:], acc[s][:, cols], SILU, bias=b_col[:])
                turned = psum.tile([P, 2, N], F32, name=f"turned{(s % 2)}_{h}")
                for t in range(2):
                    nc.tensor.transpose(turned[:, t, :], act[:, 128 * t : 128 * (t + 1)], ident[:])
                res = keep.tile([P, 2, N], F32, name=f"res{s}_{h}")
                copy_out(res[:], turned[:])
                rows = out[SLICE * s + 256 * h : SLICE * s + 256 * (h + 1), :]
                nc.sync.dma_start(out=rows.rearrange("(t p) n -> p t n", p=P), in_=res[:])

        for s in range(3):
            nc.vector.tensor_copy(
                codes1[:, SLICE * s : SLICE * (s + 1)],
                words1[:].bitcast(U32).indirect(list1[:, SLICE // 16 * s : SLICE // 16 * (s + 1)]),
            )
            pass1(s)
            finish(s, nc.vector.tensor_copy if s == 2 else nc.scalar.copy)
